import numpy as np
import ml_dtypes


def mxq(x, axis, fmt="e4m3"):
    dtype, down = {"e4m3": (ml_dtypes.float8_e4m3fn, 7), "e5m2": (ml_dtypes.float8_e5m2, 14)}[fmt]
    v = np.moveaxis(np.asarray(x, np.float32).astype(ml_dtypes.bfloat16).astype(np.float64), axis, -1)
    blocks = v.reshape(v.shape[:-1] + (-1, 32))
    amax = np.abs(blocks).max(-1, keepdims=True)
    byte = np.maximum(np.where(amax > 0, np.frexp(amax)[1] - 1 + 127, 0) - down, 1)
    scale = np.exp2(byte - 127.0)
    codes = (blocks / scale).astype(np.float32).astype(dtype).astype(np.float64)
    return np.moveaxis((codes * scale).reshape(v.shape), -1, axis)


WIDE = False


def mx_kscale(k):
    if not WIDE:
        return np.ones(k)
    levels = np.array([10, -10, 5, -5, 0])
    if k % 512:
        return np.exp2(np.random.permutation(np.resize(levels, k // 32))).repeat(32)
    a = np.empty((k // 512, 16))
    for p in range(k // 512):
        a[p, :8] = np.random.permutation(np.resize(levels, 8))
        for g in range(8):
            far = levels[np.abs(levels - a[p, g]) >= 10]
            a[p, g + 8] = far[np.random.randint(len(far))]
    return np.exp2(a.ravel()).repeat(32)


def f64(x):
    return np.asarray(x).astype(np.float64)


def striped(idx):
    return np.tile(np.asarray(idx).reshape(-1, 16).T, (8, 1)).astype(np.uint16)


def unstriped(offs):
    return offs[:16].T.reshape(-1).astype(np.int64)


E2M1 = np.array([0.0, 0.5, 1.0, 1.5, 2.0, 3.0, 4.0, 6.0, -0.0, -0.5, -1.0, -1.5, -2.0, -3.0, -4.0, -6.0])


def pack_weight(w, fmt):
    k, n = w.shape
    w = f64(np.asarray(w, np.float32).astype(ml_dtypes.bfloat16)).reshape(k // 32, 32, n)
    amax = np.abs(w).max(1)
    if fmt == "e4m3":
        byte = np.frexp(amax)[1] - 1 + 127 - 7
    else:
        mant, ex = np.frexp(amax / 6.0)
        byte = np.where(mant > 0.5, ex, ex - 1) + 127
    byte = np.clip(np.where(amax > 0, byte, 1), 1, 254)
    scaled = (w * np.exp2(127.0 - byte)[:, None, :]).reshape(k, n).astype(np.float32)
    by_word = np.ascontiguousarray(scaled.reshape(k // 512, 128, 4, n).transpose(0, 1, 3, 2))
    if fmt == "e4m3":
        words = by_word.astype(ml_dtypes.float8_e4m3fn).view(np.uint8)
    else:
        c = by_word.astype(ml_dtypes.float4_e2m1fn).view(np.uint8) & 0xF
        words = (c[..., 0::2] | (c[..., 1::2] << 4)).reshape(k // 512, 128, 2 * n)
    return np.ascontiguousarray(words), np.ascontiguousarray(byte.astype(np.uint8).reshape(k // 512, 16, n))


def unpack_weight(words, scales, fmt):
    g, _, n = scales.shape
    words = np.ascontiguousarray(words).reshape(g, 128, n, -1)
    if fmt == "e4m3":
        vals = words.view(ml_dtypes.float8_e4m3fn).astype(np.float64)
    else:
        nib = np.empty((g, 128, n, 4), np.uint8)
        nib[..., 0::2] = words & 0xF
        nib[..., 1::2] = words >> 4
        vals = E2M1[nib]
    vals = vals * np.repeat(np.exp2(scales.astype(np.float64) - 127.0), 8, axis=1)[..., None]
    return vals.transpose(0, 1, 3, 2).reshape(g * 512, n)


D, T, I, Q, E, Z, C = 512, 2048, 512, 512, 512, 1024, 256


def setup_inputs():
    n = np.random.standard_normal
    idx = np.random.permutation(T)[:I]
    idx2 = np.random.permutation(Z)[:I]
    idx3 = np.random.permutation(Q)[:C]
    fd = mx_kscale(D)
    fi = mx_kscale(I)
    ti = np.ones(T)
    ti[idx] = fi
    keysp = pack_weight(n((D, T)) / fd[:, None], "e4m3")
    return {
        "query": (n((D, Q)) * 1.0 / np.sqrt(D) * fd[:, None]).astype(np.float32),
        "keys_words": keysp[0],
        "keys_scales": keysp[1],
        "earl": (np.random.uniform(0.3, 1.7, (Q, Z))).astype(np.float32),
        "os": (np.random.uniform(0.02, 0.08, (1, I)) * fi).astype(np.float32),
        "vals": (n((E, T)) / ti).astype(np.float32),
        "pgain": (np.random.uniform(0.5, 2.0, (1, C))).astype(np.float32),
        "offs": striped(idx),
        "offs2": striped(idx2),
        "offs3": striped(idx3),
    }


def reference(query, keys_words, keys_scales, earl, os, vals, pgain, offs, offs2, offs3):
    idx = unstriped(offs)
    idx2 = unstriped(offs2)
    idx3 = unstriped(offs3)
    keysu = unpack_weight(keys_words, keys_scales, "e4m3")
    queryq = mxq(f64(query), 0, "e4m3")
    keysidxg = keysu[:, idx]
    a = queryq.T @ keysidxg
    w = a * f64(earl)[:, idx2]
    wo1 = w * f64(os)
    wt1 = wo1.T
    vt1 = f64(vals)[:, idx].T
    vt1q = mxq(vt1, 0, "e4m3")
    wt1q = mxq(wt1, 0, "e4m3")
    o = vt1q.T @ wt1q
    y = o[:, idx3] * f64(pgain)
    return y

@@ -1,0 +1,174 @@
+from contextlib import ExitStack
+
+import concourse.mybir as mybir
+from concourse.masks import make_identity
+
+D, T, I, Q, E, Z, C = 512, 2048, 512, 512, 512, 1024, 256
+FLOPS = 2 * D * Q * I + 2 * I * E * Q
+
+F32 = mybir.dt.float32
+BF16 = mybir.dt.bfloat16
+I32 = mybir.dt.int32
+U32 = mybir.dt.uint32
+U16 = mybir.dt.uint16
+U8 = mybir.dt.uint8
+FP8X4 = mybir.dt.float8_e4m3fn_x4
+MULT = mybir.AluOpType.mult
+COPY = mybir.ActivationFunctionType.Copy
+
+P = 128
+PACK = 4
+
+
+def tile_attend_earliertable_pickedout_lean_kernel(
+    tc, query, keys_words, keys_scales, earl, slot_factor, vals, pgain, offs, offs2, offs3, out
+):
+    nc = tc.nc
+    with ExitStack() as ctx:
+        sb = ctx.enter_context(tc.tile_pool(name="sb", bufs=1))
+        ps = ctx.enter_context(tc.psum_pool(name="ps", bufs=2))
+
+        token_list = sb.tile([P, I // 16], U16, name="token_list")
+        earl_list = sb.tile([P, I // 16], U16, name="earl_list")
+        pick_list = sb.tile([P, C // 16], U16, name="pick_list")
+        q_raw = sb.tile([P, PACK, Q], F32, name="q_raw")
+        key_pool = sb.tile([P, T], U32, name="key_pool")
+        key_scale_pool = sb.tile([P, T], U8, name="key_scale_pool", align_bytes=64)
+        earl_rows = [sb.tile([P, Z], F32, name="earl_rows%d" % j, align_bytes=64) for j in range(Q // P)]
+        val_rows = [sb.tile([P, T], F32, name="val_rows%d" % j) for j in range(E // P)]
+        factor_cols = sb.tile([P, I // P], F32, name="factor_cols")
+        gain_cols = sb.tile([P, C // P], F32, name="gain_cols")
+
+        nc.gpsimd.memset(key_scale_pool[:].bitcast(I32), 0)
+        nc.sync.dma_start(out=q_raw[:], in_=query.rearrange("(p t) q -> p t q", t=PACK))
+        nc.sync.dma_start(token_list[:], offs)
+        for quad in range(4):
+            nc.sync.dma_start(
+                out=key_scale_pool[32 * quad : 32 * quad + 4, :].bitcast(I32),
+                in_=keys_scales[0, 4 * quad : 4 * quad + 4, :].bitcast(I32),
+            )
+        nc.sync.dma_start(out=factor_cols[:], in_=slot_factor.rearrange("o (p j) -> (o p) j", p=P))
+        nc.sync.dma_start(
+            out=key_pool[:].bitcast(I32), in_=keys_words[0].rearrange("p n t -> p (n t)").bitcast(I32)
+        )
+        nc.sync.dma_start(out=earl_rows[0][:], in_=earl[0:P, :])
+        nc.sync.dma_start(earl_list[:], offs2)
+        for j in range(1, Q // P):
+            nc.sync.dma_start(out=earl_rows[j][:], in_=earl[j * P : (j + 1) * P, :])
+        nc.sync.dma_start(out=val_rows[0][:], in_=vals[0:P, :])
+        nc.sync.dma_start(out=gain_cols[:], in_=pgain.rearrange("o (p j) -> (o p) j", p=P))
+        nc.sync.dma_start(pick_list[:], offs3)
+        for j in range(1, E // P):
+            nc.sync.dma_start(out=val_rows[j][:], in_=vals[j * P : (j + 1) * P, :])
+
+        identity = sb.tile([P, P], F32, name="identity")
+        make_identity(nc, identity[:])
+
+        def spread_row(cols, name):
+            n = cols.shape[1]
+            bank = ps.tile([P, n, P], F32, name="bank_" + name, tag="turn", bufs=4)
+            for j in range(n):
+                nc.tensor.transpose(bank[:, j, :], cols[:, j : j + 1].to_broadcast([P, P]), identity[:])
+            row = sb.tile([P, P, n], F32, name=name)
+            nc.scalar.copy(out=row[:], in_=bank[:].rearrange("p j m -> p m j"))
+            return row[:].rearrange("p m j -> p (m j)")
+
+        factor_row = spread_row(factor_cols[:], "factor_row")
+
+        key_scales = sb.tile([P, I], U8, name="key_scales", align_bytes=64)
+        nc.vector.tensor_copy(key_scales[:], key_scale_pool[:].indirect(token_list[:]))
+
+        q_grouped = sb.tile([P, Q, PACK], BF16, name="q_grouped", align_bytes=64)
+        for copy, cols in ((nc.vector.tensor_copy, slice(0, P)), (nc.scalar.copy, slice(P, Q))):
+            copy(
+                out=q_grouped[:, cols, :].rearrange("p (c i) t -> p c t i", i=4),
+                in_=q_raw[:, :, cols].rearrange("p t (c i) -> p c t i", i=4),
+            )
+        q_codes = sb.tile([P, Q], U32, name="q_codes", tag="key_scale_pool", align_bytes=64)
+        q_scales = sb.tile([P, Q], U8, name="q_scales", align_bytes=64)
+        nc.vector.quantize_mx(
+            out=q_codes[:].bitcast(FP8X4), scales=q_scales[:], in_=q_grouped[:].rearrange("p q t -> p (q t)")
+        )
+
+        key_codes = sb.tile([P, I], U32, name="key_codes", align_bytes=64)
+        nc.vector.tensor_copy(key_codes[:], key_pool[:].indirect(token_list[:]))
+
+        def turn_and_quantize(rows, grouped, codes, scales, name):
+            words = rows.bitcast(F32)
+            bank = ps.tile([P, 2, P], F32, name="bank_" + name, tag="turn", bufs=4)
+            for u in range(2):
+                nc.tensor.transpose(bank[:, u, :], words[:, u : I // 2 : 2], identity[:])
+            nc.scalar.copy(out=grouped.rearrange("p (r u) -> p r u", u=2), in_=bank[:].rearrange("p u r -> p r u"))
+            nc.vector.quantize_mx(out=codes.bitcast(FP8X4), scales=scales, in_=grouped.bitcast(BF16))
+
+        w_codes = sb.tile([P, Q], U32, name="w_codes", align_bytes=64)
+        w_scales = sb.tile([P, Q], U8, name="w_scales", align_bytes=64)
+        weight_rows = []
+        for j in range(Q // P):
+            cols = slice(j * P, (j + 1) * P)
+            scores = ps.tile([P, I], F32, name="scores%d" % j, tag="scores")
+            nc.tensor.matmul_mx(
+                out=scores[:],
+                lhsT=q_codes[:, cols].bitcast(FP8X4),
+                lhsT_scale=q_scales[:, cols],
+                rhs=key_codes[:].bitcast(FP8X4),
+                rhs_scale=key_scales[:],
+                start=True,
+                stop=True,
+            )
+            scaled = sb.tile([P, I], F32, name="scaled%d" % j)
+            nc.vector.tensor_tensor(scaled[:], scores[:], factor_row, MULT)
+            earl_picked = sb.tile([P, I], F32, name="earl_picked%d" % j)
+            nc.scalar.activation(earl_picked[:], earl_rows[j][:].indirect(earl_list[:]), COPY)
+            weights = sb.tile([P, I], BF16, name="weights%d" % j)
+            nc.vector.tensor_tensor(weights[:], scaled[:], earl_picked[:], MULT)
+            weight_rows.append(weights)
+        w_grouped = sb.tile([P, 2 * Q], F32, name="w_grouped", tag="earl_rows3", align_bytes=64)
+        for j in range(Q // P):
+            cols = slice(j * P, (j + 1) * P)
+            turn_and_quantize(
+                weight_rows[j][:], w_grouped[:, 2 * j * P : 2 * (j + 1) * P], w_codes[:, cols], w_scales[:, cols], "w%d" % j
+            )
+
+        half = I // 2
+        blocks = E // P
+        sums = {}
+        o_rows = {}
+
+        def multiply(j):
+            picked = sb.tile([P, I], BF16, name="val_picked%d" % j)
+            nc.vector.tensor_copy(picked[:, :half], val_rows[j][:].indirect(token_list[:, : half // 16]))
+            nc.scalar.activation(picked[:, half:], val_rows[j][:].indirect(token_list[:, half // 16 :]), COPY)
+            v_grouped = sb.tile([P, 2 * P], F32, name="v_grouped%d" % j, align_bytes=64)
+            v_codes = sb.tile([P, P], U32, name="v_codes%d" % j, align_bytes=64)
+            v_scales = sb.tile([P, P], U8, name="v_scales%d" % j, align_bytes=64)
+            turn_and_quantize(picked[:], v_grouped[:], v_codes[:], v_scales[:], "v%d" % j)
+            sums[j] = ps.tile([P, Q], F32, name="sums%d" % j, tag="sums")
+            nc.tensor.matmul_mx(
+                out=sums[j][:],
+                lhsT=v_codes[:].bitcast(FP8X4),
+                lhsT_scale=v_scales[:],
+                rhs=w_codes[:].bitcast(FP8X4),
+                rhs_scale=w_scales[:],
+                start=True,
+                stop=True,
+            )
+
+        def copy_out(j):
+            o_rows[j] = sb.tile([P, Q], F32, name="o_rows%d" % j, tag="val_picked%d" % (j + 1))
+            nc.scalar.copy(out=o_rows[j][:], in_=sums[j][:])
+
+        def pick_and_store(j):
+            result = sb.tile([P, C], F32, name="result%d" % j, tag="val_rows%d" % (j + 2))
+            nc.vector.tensor_tensor(result[:], o_rows[j][:].indirect(pick_list[:]), gain_row, MULT)
+            nc.sync.dma_start(out=out[j * P : (j + 1) * P, :], in_=result[:])
+
+        multiply(0)
+        gain_row = spread_row(gain_cols[:], "gain_row")
+        for j in range(1, blocks + 2):
+            if j < blocks:
+                multiply(j)
+            if j - 1 < blocks:
+                copy_out(j - 1)
+            if j >= 2:
+                pick_and_store(j - 2)

@@ -18,6 +18,7 @@ COPY = mybir.ActivationFunctionType.Copy
 
 P = 128
 PACK = 4
+VAL_BYTES = 4 * T
 
 
 def tile_attend_earliertable_pickedout_lean_kernel(
@@ -26,7 +27,8 @@ def tile_attend_earliertable_pickedout_lean_kernel(
     nc = tc.nc
     with ExitStack() as ctx:
         sb = ctx.enter_context(tc.tile_pool(name="sb", bufs=1))
-        ps = ctx.enter_context(tc.psum_pool(name="ps", bufs=2))
+        reuse = ctx.enter_context(tc.tile_pool(name="reuse", bufs=1))
+        ps = ctx.enter_context(tc.psum_pool(name="ps", bufs=4))
 
         token_list = sb.tile([P, I // 16], U16, name="token_list")
         earl_list = sb.tile([P, I // 16], U16, name="earl_list")
@@ -35,7 +37,9 @@ def tile_attend_earliertable_pickedout_lean_kernel(
         key_pool = sb.tile([P, T], U32, name="key_pool")
         key_scale_pool = sb.tile([P, T], U8, name="key_scale_pool", align_bytes=64)
         earl_rows = [sb.tile([P, Z], F32, name="earl_rows%d" % j, align_bytes=64) for j in range(Q // P)]
-        val_rows = [sb.tile([P, T], F32, name="val_rows%d" % j) for j in range(E // P)]
+        val_rows = [
+            reuse.tile([P, T], F32, name="val_rows%d" % j, offset=j * VAL_BYTES, align_bytes=64) for j in range(E // P)
+        ]
         factor_cols = sb.tile([P, I // P], F32, name="factor_cols")
         gain_cols = sb.tile([P, C // P], F32, name="gain_cols")
 
@@ -66,7 +70,7 @@ def tile_attend_earliertable_pickedout_lean_kernel(
 
         def spread_row(cols, name):
             n = cols.shape[1]
-            bank = ps.tile([P, n, P], F32, name="bank_" + name, tag="turn", bufs=4)
+            bank = ps.tile([P, n, P], F32, name="bank_" + name, tag="products")
             for j in range(n):
                 nc.tensor.transpose(bank[:, j, :], cols[:, j : j + 1].to_broadcast([P, P]), identity[:])
             row = sb.tile([P, P, n], F32, name=name)
@@ -93,20 +97,23 @@ def tile_attend_earliertable_pickedout_lean_kernel(
         key_codes = sb.tile([P, I], U32, name="key_codes", align_bytes=64)
         nc.vector.tensor_copy(key_codes[:], key_pool[:].indirect(token_list[:]))
 
-        def turn_and_quantize(rows, grouped, codes, scales, name):
+        def turn(rows, name):
             words = rows.bitcast(F32)
-            bank = ps.tile([P, 2, P], F32, name="bank_" + name, tag="turn", bufs=4)
+            bank = ps.tile([P, 2, P], F32, name="bank_" + name, tag="turn")
             for u in range(2):
                 nc.tensor.transpose(bank[:, u, :], words[:, u : I // 2 : 2], identity[:])
-            nc.scalar.copy(out=grouped.rearrange("p (r u) -> p r u", u=2), in_=bank[:].rearrange("p u r -> p r u"))
+            return bank
+
+        def group_and_quantize(copy, bank, grouped, codes, scales):
+            copy(out=grouped.rearrange("p (r u) -> p r u", u=2), in_=bank[:].rearrange("p u r -> p r u"))
             nc.vector.quantize_mx(out=codes.bitcast(FP8X4), scales=scales, in_=grouped.bitcast(BF16))
 
         w_codes = sb.tile([P, Q], U32, name="w_codes", align_bytes=64)
         w_scales = sb.tile([P, Q], U8, name="w_scales", align_bytes=64)
-        weight_rows = []
+        weight_banks = []
         for j in range(Q // P):
             cols = slice(j * P, (j + 1) * P)
-            scores = ps.tile([P, I], F32, name="scores%d" % j, tag="scores")
+            scores = ps.tile([P, I], F32, name="scores%d" % j, tag="products")
             nc.tensor.matmul_mx(
                 out=scores[:],
                 lhsT=q_codes[:, cols].bitcast(FP8X4),
@@ -122,28 +129,47 @@ def tile_attend_earliertable_pickedout_lean_kernel(
             nc.scalar.activation(earl_picked[:], earl_rows[j][:].indirect(earl_list[:]), COPY)
             weights = sb.tile([P, I], BF16, name="weights%d" % j)
             nc.vector.tensor_tensor(weights[:], scaled[:], earl_picked[:], MULT)
-            weight_rows.append(weights)
+            weight_banks.append(turn(weights[:], "w%d" % j))
         w_grouped = sb.tile([P, 2 * Q], F32, name="w_grouped", tag="earl_rows3", align_bytes=64)
         for j in range(Q // P):
             cols = slice(j * P, (j + 1) * P)
-            turn_and_quantize(
-                weight_rows[j][:], w_grouped[:, 2 * j * P : 2 * (j + 1) * P], w_codes[:, cols], w_scales[:, cols], "w%d" % j
+            group_and_quantize(
+                nc.vector.tensor_copy,
+                weight_banks[j],
+                w_grouped[:, 2 * j * P : 2 * (j + 1) * P],
+                w_codes[:, cols],
+                w_scales[:, cols],
             )
+
+        gain_row = spread_row(gain_cols[:], "gain_row")
 
         half = I // 2
         blocks = E // P
+        val_banks = {}
+        v_grouped = {}
         sums = {}
         o_rows = {}
 
-        def multiply(j):
+        def over_val_rows(j, place, shape, name):
+            if j < blocks:
+                return reuse.tile(shape, F32, name=name, offset=j * VAL_BYTES + place * 2048, align_bytes=64)
+            return sb.tile(shape, F32, name=name, align_bytes=64)
+
+        def gather(j):
             picked = sb.tile([P, I], BF16, name="val_picked%d" % j)
-            nc.vector.tensor_copy(picked[:, :half], val_rows[j][:].indirect(token_list[:, : half // 16]))
-            nc.scalar.activation(picked[:, half:], val_rows[j][:].indirect(token_list[:, half // 16 :]), COPY)
-            v_grouped = sb.tile([P, 2 * P], F32, name="v_grouped%d" % j, align_bytes=64)
+            if j < 2:
+                nc.scalar.activation(picked[:], val_rows[j][:].indirect(token_list[:]), COPY)
+            else:
+                nc.vector.tensor_copy(picked[:, :half], val_rows[j][:].indirect(token_list[:, : half // 16]))
+                nc.scalar.activation(picked[:, half:], val_rows[j][:].indirect(token_list[:, half // 16 :]), COPY)
+            val_banks[j] = turn(picked[:], "v%d" % j)
+
+        def multiply(j):
+            v_grouped[j] = over_val_rows(j + 1, 0, [P, 2 * P], "v_grouped%d" % j)
             v_codes = sb.tile([P, P], U32, name="v_codes%d" % j, align_bytes=64)
             v_scales = sb.tile([P, P], U8, name="v_scales%d" % j, align_bytes=64)
-            turn_and_quantize(picked[:], v_grouped[:], v_codes[:], v_scales[:], "v%d" % j)
-            sums[j] = ps.tile([P, Q], F32, name="sums%d" % j, tag="sums")
+            group_and_quantize(nc.scalar.copy, val_banks[j], v_grouped[j][:], v_codes[:], v_scales[:])
+            sums[j] = ps.tile([P, Q], F32, name="sums%d" % j, tag="products")
             nc.tensor.matmul_mx(
                 out=sums[j][:],
                 lhsT=v_codes[:].bitcast(FP8X4),
@@ -155,20 +181,18 @@ def tile_attend_earliertable_pickedout_lean_kernel(
             )
 
         def copy_out(j):
-            o_rows[j] = sb.tile([P, Q], F32, name="o_rows%d" % j, tag="val_picked%d" % (j + 1))
+            o_rows[j] = over_val_rows(j + 2, 1, [P, Q], "o_rows%d" % j)
             nc.scalar.copy(out=o_rows[j][:], in_=sums[j][:])
 
         def pick_and_store(j):
-            result = sb.tile([P, C], F32, name="result%d" % j, tag="val_rows%d" % (j + 2))
+            if j == 1:
+                result = sb.tile([P, C], F32, name="result%d" % j, tag="v_grouped3", align_bytes=64)
+            else:
+                result = over_val_rows(j + 3, 2, [P, C], "result%d" % j)
             nc.vector.tensor_tensor(result[:], o_rows[j][:].indirect(pick_list[:]), gain_row, MULT)
             nc.sync.dma_start(out=out[j * P : (j + 1) * P, :], in_=result[:])
 
-        multiply(0)
-        gain_row = spread_row(gain_cols[:], "gain_row")
-        for j in range(1, blocks + 2):
-            if j < blocks:
-                multiply(j)
-            if j - 1 < blocks:
-                copy_out(j - 1)
-            if j >= 2:
-                pick_and_store(j - 2)
+        for step in range(blocks + 3):
+            for lag, stage in enumerate((gather, multiply, copy_out, pick_and_store)):
+                if 0 <= step - lag < blocks:
+                    stage(step - lag)

@@ -36,7 +36,7 @@ def tile_attend_earliertable_pickedout_lean_kernel(
         q_raw = sb.tile([P, PACK, Q], F32, name="q_raw")
         key_pool = sb.tile([P, T], U32, name="key_pool")
         key_scale_pool = sb.tile([P, T], U8, name="key_scale_pool", align_bytes=64)
-        earl_rows = [sb.tile([P, Z], F32, name="earl_rows%d" % j, align_bytes=64) for j in range(Q // P)]
+        earl_pairs = [sb.tile([P, 2, Z], F32, name="earl_pair%d" % h, align_bytes=64) for h in range(2)]
         val_rows = [
             reuse.tile([P, T], F32, name="val_rows%d" % j, offset=j * VAL_BYTES, align_bytes=64) for j in range(E // P)
         ]
@@ -55,15 +55,14 @@ def tile_attend_earliertable_pickedout_lean_kernel(
         nc.sync.dma_start(
             out=key_pool[:].bitcast(I32), in_=keys_words[0].rearrange("p n t -> p (n t)").bitcast(I32)
         )
-        nc.sync.dma_start(out=earl_rows[0][:], in_=earl[0:P, :])
+        nc.sync.dma_start(out=earl_pairs[0][:], in_=earl[: Q // 2, :].rearrange("(j p) z -> p j z", p=P))
         nc.sync.dma_start(earl_list[:], offs2)
-        for j in range(1, Q // P):
-            nc.sync.dma_start(out=earl_rows[j][:], in_=earl[j * P : (j + 1) * P, :])
+        nc.sync.dma_start(out=earl_pairs[1][:], in_=earl[Q // 2 :, :].rearrange("(j p) z -> p j z", p=P))
         nc.sync.dma_start(out=val_rows[0][:], in_=vals[0:P, :])
         nc.sync.dma_start(out=gain_cols[:], in_=pgain.rearrange("o (p j) -> (o p) j", p=P))
-        nc.sync.dma_start(pick_list[:], offs3)
         for j in range(1, E // P):
             nc.sync.dma_start(out=val_rows[j][:], in_=vals[j * P : (j + 1) * P, :])
+        nc.sync.dma_start(pick_list[:], offs3)
 
         identity = sb.tile([P, P], F32, name="identity")
         make_identity(nc, identity[:])
@@ -126,11 +125,11 @@ def tile_attend_earliertable_pickedout_lean_kernel(
             scaled = sb.tile([P, I], F32, name="scaled%d" % j)
             nc.vector.tensor_tensor(scaled[:], scores[:], factor_row, MULT)
             earl_picked = sb.tile([P, I], F32, name="earl_picked%d" % j)
-            nc.scalar.activation(earl_picked[:], earl_rows[j][:].indirect(earl_list[:]), COPY)
+            nc.scalar.activation(earl_picked[:], earl_pairs[j // 2][:, j % 2, :].indirect(earl_list[:]), COPY)
             weights = sb.tile([P, I], BF16, name="weights%d" % j)
             nc.vector.tensor_tensor(weights[:], scaled[:], earl_picked[:], MULT)
             weight_banks.append(turn(weights[:], "w%d" % j))
-        w_grouped = sb.tile([P, 2 * Q], F32, name="w_grouped", tag="earl_rows3", align_bytes=64)
+        w_grouped = sb.tile([P, 2 * Q], F32, name="w_grouped", tag="earl_pair1", align_bytes=64)
         for j in range(Q // P):
             cols = slice(j * P, (j + 1) * P)
             group_and_quantize(

from contextlib import ExitStack

import concourse.mybir as mybir
from concourse.masks import make_identity

D, T, I, Q, E, Z, C = 512, 2048, 512, 512, 512, 1024, 256
FLOPS = 2 * D * Q * I + 2 * I * E * Q

F32 = mybir.dt.float32
BF16 = mybir.dt.bfloat16
I32 = mybir.dt.int32
U32 = mybir.dt.uint32
U16 = mybir.dt.uint16
U8 = mybir.dt.uint8
FP8X4 = mybir.dt.float8_e4m3fn_x4
MULT = mybir.AluOpType.mult
COPY = mybir.ActivationFunctionType.Copy

P = 128
PACK = 4
VAL_BYTES = 4 * T


def tile_attend_earliertable_pickedout_lean_kernel(
    tc, query, keys_words, keys_scales, earl, slot_factor, vals, pgain, offs, offs2, offs3, out
):
    nc = tc.nc
    with ExitStack() as ctx:
        sb = ctx.enter_context(tc.tile_pool(name="sb", bufs=1))
        reuse = ctx.enter_context(tc.tile_pool(name="reuse", bufs=1))
        ps = ctx.enter_context(tc.psum_pool(name="ps", bufs=4))

        token_list = sb.tile([P, I // 16], U16, name="token_list")
        earl_list = sb.tile([P, I // 16], U16, name="earl_list")
        pick_list = sb.tile([P, C // 16], U16, name="pick_list")
        q_raw = sb.tile([P, PACK, Q], F32, name="q_raw")
        key_pool = sb.tile([P, T], U32, name="key_pool")
        key_scale_pool = sb.tile([P, T], U8, name="key_scale_pool", align_bytes=64)
        earl_pairs = [sb.tile([P, 2, Z], F32, name="earl_pair%d" % h, align_bytes=64) for h in range(2)]
        val_rows = [
            reuse.tile([P, T], F32, name="val_rows%d" % j, offset=j * VAL_BYTES, align_bytes=64) for j in range(E // P)
        ]
        factor_cols = sb.tile([P, I // P], F32, name="factor_cols")
        gain_cols = sb.tile([P, C // P], F32, name="gain_cols")

        nc.gpsimd.memset(key_scale_pool[:].bitcast(I32), 0)
        nc.sync.dma_start(out=q_raw[:], in_=query.rearrange("(p t) q -> p t q", t=PACK))
        nc.sync.dma_start(token_list[:], offs)
        for quad in range(4):
            nc.sync.dma_start(
                out=key_scale_pool[32 * quad : 32 * quad + 4, :].bitcast(I32),
                in_=keys_scales[0, 4 * quad : 4 * quad + 4, :].bitcast(I32),
            )
        nc.sync.dma_start(out=factor_cols[:], in_=slot_factor.rearrange("o (p j) -> (o p) j", p=P))
        nc.sync.dma_start(
            out=key_pool[:].bitcast(I32), in_=keys_words[0].rearrange("p n t -> p (n t)").bitcast(I32)
        )
        nc.sync.dma_start(out=earl_pairs[0][:], in_=earl[: Q // 2, :].rearrange("(j p) z -> p j z", p=P))
        nc.sync.dma_start(earl_list[:], offs2)
        nc.sync.dma_start(out=earl_pairs[1][:], in_=earl[Q // 2 :, :].rearrange("(j p) z -> p j z", p=P))
        nc.sync.dma_start(out=val_rows[0][:], in_=vals[0:P, :])
        nc.sync.dma_start(out=gain_cols[:], in_=pgain.rearrange("o (p j) -> (o p) j", p=P))
        for j in range(1, E // P):
            nc.sync.dma_start(out=val_rows[j][:], in_=vals[j * P : (j + 1) * P, :])
        nc.sync.dma_start(pick_list[:], offs3)

        identity = sb.tile([P, P], F32, name="identity")
        make_identity(nc, identity[:])

        def spread_row(cols, name):
            n = cols.shape[1]
            bank = ps.tile([P, n, P], F32, name="bank_" + name, tag="products")
            for j in range(n):
                nc.tensor.transpose(bank[:, j, :], cols[:, j : j + 1].to_broadcast([P, P]), identity[:])
            row = sb.tile([P, P, n], F32, name=name)
            nc.scalar.copy(out=row[:], in_=bank[:].rearrange("p j m -> p m j"))
            return row[:].rearrange("p m j -> p (m j)")

        factor_row = spread_row(factor_cols[:], "factor_row")

        key_scales = sb.tile([P, I], U8, name="key_scales", align_bytes=64)
        nc.vector.tensor_copy(key_scales[:], key_scale_pool[:].indirect(token_list[:]))

        q_grouped = sb.tile([P, Q, PACK], BF16, name="q_grouped", align_bytes=64)
        for copy, cols in ((nc.vector.tensor_copy, slice(0, P)), (nc.scalar.copy, slice(P, Q))):
            copy(
                out=q_grouped[:, cols, :].rearrange("p (c i) t -> p c t i", i=4),
                in_=q_raw[:, :, cols].rearrange("p t (c i) -> p c t i", i=4),
            )
        q_codes = sb.tile([P, Q], U32, name="q_codes", tag="key_scale_pool", align_bytes=64)
        q_scales = sb.tile([P, Q], U8, name="q_scales", align_bytes=64)
        nc.vector.quantize_mx(
            out=q_codes[:].bitcast(FP8X4), scales=q_scales[:], in_=q_grouped[:].rearrange("p q t -> p (q t)")
        )

        key_codes = sb.tile([P, I], U32, name="key_codes", align_bytes=64)
        nc.vector.tensor_copy(key_codes[:], key_pool[:].indirect(token_list[:]))

        def turn(rows, name):
            words = rows.bitcast(F32)
            bank = ps.tile([P, 2, P], F32, name="bank_" + name, tag="turn")
            for u in range(2):
                nc.tensor.transpose(bank[:, u, :], words[:, u : I // 2 : 2], identity[:])
            return bank

        def group_and_quantize(copy, bank, grouped, codes, scales):
            copy(out=grouped.rearrange("p (r u) -> p r u", u=2), in_=bank[:].rearrange("p u r -> p r u"))
            nc.vector.quantize_mx(out=codes.bitcast(FP8X4), scales=scales, in_=grouped.bitcast(BF16))

        w_codes = sb.tile([P, Q], U32, name="w_codes", align_bytes=64)
        w_scales = sb.tile([P, Q], U8, name="w_scales", align_bytes=64)
        weight_banks = []
        for j in range(Q // P):
            cols = slice(j * P, (j + 1) * P)
            scores = ps.tile([P, I], F32, name="scores%d" % j, tag="products")
            nc.tensor.matmul_mx(
                out=scores[:],
                lhsT=q_codes[:, cols].bitcast(FP8X4),
                lhsT_scale=q_scales[:, cols],
                rhs=key_codes[:].bitcast(FP8X4),
                rhs_scale=key_scales[:],
                start=True,
                stop=True,
            )
            scaled = sb.tile([P, I], F32, name="scaled%d" % j)
            nc.vector.tensor_tensor(scaled[:], scores[:], factor_row, MULT)
            earl_picked = sb.tile([P, I], F32, name="earl_picked%d" % j)
            nc.scalar.activation(earl_picked[:], earl_pairs[j // 2][:, j % 2, :].indirect(earl_list[:]), COPY)
            weights = sb.tile([P, I], BF16, name="weights%d" % j)
            nc.vector.tensor_tensor(weights[:], scaled[:], earl_picked[:], MULT)
            weight_banks.append(turn(weights[:], "w%d" % j))
        w_grouped = sb.tile([P, 2 * Q], F32, name="w_grouped", tag="earl_pair1", align_bytes=64)
        for j in range(Q // P):
            cols = slice(j * P, (j + 1) * P)
            group_and_quantize(
                nc.vector.tensor_copy,
                weight_banks[j],
                w_grouped[:, 2 * j * P : 2 * (j + 1) * P],
                w_codes[:, cols],
                w_scales[:, cols],
            )

        gain_row = spread_row(gain_cols[:], "gain_row")

        half = I // 2
        blocks = E // P
        val_banks = {}
        v_grouped = {}
        sums = {}
        o_rows = {}

        def over_val_rows(j, place, shape, name):
            if j < blocks:
                return reuse.tile(shape, F32, name=name, offset=j * VAL_BYTES + place * 2048, align_bytes=64)
            return sb.tile(shape, F32, name=name, align_bytes=64)

        def gather(j):
            picked = sb.tile([P, I], BF16, name="val_picked%d" % j)
            if j < 2:
                nc.scalar.activation(picked[:], val_rows[j][:].indirect(token_list[:]), COPY)
            else:
                nc.vector.tensor_copy(picked[:, :half], val_rows[j][:].indirect(token_list[:, : half // 16]))
                nc.scalar.activation(picked[:, half:], val_rows[j][:].indirect(token_list[:, half // 16 :]), COPY)
            val_banks[j] = turn(picked[:], "v%d" % j)

        def multiply(j):
            v_grouped[j] = over_val_rows(j + 1, 0, [P, 2 * P], "v_grouped%d" % j)
            v_codes = sb.tile([P, P], U32, name="v_codes%d" % j, align_bytes=64)
            v_scales = sb.tile([P, P], U8, name="v_scales%d" % j, align_bytes=64)
            group_and_quantize(nc.scalar.copy, val_banks[j], v_grouped[j][:], v_codes[:], v_scales[:])
            sums[j] = ps.tile([P, Q], F32, name="sums%d" % j, tag="products")
            nc.tensor.matmul_mx(
                out=sums[j][:],
                lhsT=v_codes[:].bitcast(FP8X4),
                lhsT_scale=v_scales[:],
                rhs=w_codes[:].bitcast(FP8X4),
                rhs_scale=w_scales[:],
                start=True,
                stop=True,
            )

        def copy_out(j):
            o_rows[j] = over_val_rows(j + 2, 1, [P, Q], "o_rows%d" % j)
            nc.scalar.copy(out=o_rows[j][:], in_=sums[j][:])

        def pick_and_store(j):
            if j == 1:
                result = sb.tile([P, C], F32, name="result%d" % j, tag="v_grouped3", align_bytes=64)
            else:
                result = over_val_rows(j + 3, 2, [P, C], "result%d" % j)
            nc.vector.tensor_tensor(result[:], o_rows[j][:].indirect(pick_list[:]), gain_row, MULT)
            nc.sync.dma_start(out=out[j * P : (j + 1) * P, :], in_=result[:])

        for step in range(blocks + 3):
            for lag, stage in enumerate((gather, multiply, copy_out, pick_and_store)):
                if 0 <= step - lag < blocks:
                    stage(step - lag)
